import numpy as np
import ml_dtypes


def mxq(x, axis, fmt="e4m3"):
    dtype, down = {"e4m3": (ml_dtypes.float8_e4m3fn, 7), "e5m2": (ml_dtypes.float8_e5m2, 14)}[fmt]
    v = np.moveaxis(np.asarray(x, np.float32).astype(ml_dtypes.bfloat16).astype(np.float64), axis, -1)
    blocks = v.reshape(v.shape[:-1] + (-1, 32))
    amax = np.abs(blocks).max(-1, keepdims=True)
    byte = np.maximum(np.where(amax > 0, np.frexp(amax)[1] - 1 + 127, 0) - down, 1)
    scale = np.exp2(byte - 127.0)
    codes = (blocks / scale).astype(np.float32).astype(dtype).astype(np.float64)
    return np.moveaxis((codes * scale).reshape(v.shape), -1, axis)


WIDE = False


def mx_kscale(k):
    if not WIDE:
        return np.ones(k)
    levels = np.array([10, -10, 5, -5, 0])
    if k % 512:
        return np.exp2(np.random.permutation(np.resize(levels, k // 32))).repeat(32)
    a = np.empty((k // 512, 16))
    for p in range(k // 512):
        a[p, :8] = np.random.permutation(np.resize(levels, 8))
        for g in range(8):
            far = levels[np.abs(levels - a[p, g]) >= 10]
            a[p, g + 8] = far[np.random.randint(len(far))]
    return np.exp2(a.ravel()).repeat(32)


def f64(x):
    return np.asarray(x).astype(np.float64)


def striped8(idx):
    return np.asarray(idx).reshape(8, -1, 16).transpose(0, 2, 1).reshape(128, -1).astype(np.uint16)


def unstriped8(offs):
    return offs.reshape(8, 16, -1).transpose(0, 2, 1).reshape(8, -1).astype(np.int64)


def pick8(x, idx, run):
    r = np.arange(len(x))
    return x[r[:, None], idx[r % (8 * run) // run]]


E2M1 = np.array([0.0, 0.5, 1.0, 1.5, 2.0, 3.0, 4.0, 6.0, -0.0, -0.5, -1.0, -1.5, -2.0, -3.0, -4.0, -6.0])


def pack_weight(w, fmt):
    k, n = w.shape
    w = f64(np.asarray(w, np.float32).astype(ml_dtypes.bfloat16)).reshape(k // 32, 32, n)
    amax = np.abs(w).max(1)
    if fmt == "e4m3":
        byte = np.frexp(amax)[1] - 1 + 127 - 7
    else:
        mant, ex = np.frexp(amax / 6.0)
        byte = np.where(mant > 0.5, ex, ex - 1) + 127
    byte = np.clip(np.where(amax > 0, byte, 1), 1, 254)
    scaled = (w * np.exp2(127.0 - byte)[:, None, :]).reshape(k, n).astype(np.float32)
    by_word = np.ascontiguousarray(scaled.reshape(k // 512, 128, 4, n).transpose(0, 1, 3, 2))
    if fmt == "e4m3":
        words = by_word.astype(ml_dtypes.float8_e4m3fn).view(np.uint8)
    else:
        c = by_word.astype(ml_dtypes.float4_e2m1fn).view(np.uint8) & 0xF
        words = (c[..., 0::2] | (c[..., 1::2] << 4)).reshape(k // 512, 128, 2 * n)
    return np.ascontiguousarray(words), np.ascontiguousarray(byte.astype(np.uint8).reshape(k // 512, 16, n))


def unpack_weight(words, scales, fmt):
    g, _, n = scales.shape
    words = np.ascontiguousarray(words).reshape(g, 128, n, -1)
    if fmt == "e4m3":
        vals = words.view(ml_dtypes.float8_e4m3fn).astype(np.float64)
    else:
        nib = np.empty((g, 128, n, 4), np.uint8)
        nib[..., 0::2] = words & 0xF
        nib[..., 1::2] = words >> 4
        vals = E2M1[nib]
    vals = vals * np.repeat(np.exp2(scales.astype(np.float64) - 127.0), 8, axis=1)[..., None]
    return vals.transpose(0, 1, 3, 2).reshape(g * 512, n)


D, T, I, Q = 512, 1024, 512, 128


def setup_inputs():
    n = np.random.standard_normal
    idx = np.stack([np.random.permutation(T)[:I] for _ in range(8)])
    idx2 = np.stack([np.random.permutation(T)[:I] for _ in range(8)])
    idx4 = np.stack([np.random.permutation(T)[:I] for _ in range(8)])
    fd = mx_kscale(D)
    keysp = pack_weight(n((D, T)) / fd[:, None], "e2m1")
    return {
        "query": (n((D, Q)) * 1.0 / np.sqrt(D) * fd[:, None]).astype(np.float32),
        "query2": (n((D, Q)) * 1.0 / np.sqrt(D) * fd[:, None]).astype(np.float32),
        "keys_words": keysp[0],
        "keys_scales": keysp[1],
        "lam": (np.random.uniform(1.0, 3.0, (Q, 1))).astype(np.float32),
        "sharp": (np.random.uniform(1.5, 3.0, (Q, 1))).astype(np.float32),
        "share": (np.random.uniform(0.5, 0.9, (Q, 1))).astype(np.float32),
        "old": (np.random.uniform(0.0, 2.0, (Q, T))).astype(np.float32),
        "gainm": (np.random.uniform(0.5, 1.5, (Q, I))).astype(np.float32),
        "offs": striped8(idx),
        "offs2": striped8(idx2),
        "offs4": striped8(idx4),
    }


def reference(query, query2, keys_words, keys_scales, lam, sharp, share, old, gainm, offs, offs2, offs4):
    idx = unstriped8(offs)
    idx2 = unstriped8(offs2)
    idx4 = unstriped8(offs4)
    keysu = unpack_weight(keys_words, keys_scales, "e2m1")
    queryq = mxq(f64(query), 0, "e4m3")
    a = queryq.T @ keysu
    query2q = mxq(f64(query2), 0, "e4m3")
    b = query2q.T @ keysu
    la = np.square(pick8(a, idx, 16)) + np.square(pick8(b, idx, 16))
    lb = np.square(pick8(a, idx2, 16)) + np.square(pick8(b, idx2, 16))
    s = (pick8(a, idx, 16) * pick8(a, idx2, 16) + pick8(b, idx, 16) * pick8(b, idx2, 16)) / np.sqrt(la * lb + 0.5) * f64(lam)
    p = np.exp(s - np.max(s, axis=1, keepdims=True))
    r = p / np.sum(p, axis=1, keepdims=True)
    s2 = s * f64(sharp)
    p2 = np.exp(s2 - np.max(s2, axis=1, keepdims=True))
    r2 = p2 / np.sum(p2, axis=1, keepdims=True)
    w = r * f64(share) - r2 * (1.0 - f64(share))
    ws = w * f64(gainm) * 256.0
    wf = np.zeros((Q, T))
    wf[np.arange(Q)[:, None], idx4[np.arange(Q) % 128 // 16]] = ws
    y = f64(old) + wf
    return y

@@ -1,0 +1,165 @@
+from contextlib import ExitStack
+
+import concourse.mybir as mybir
+
+D, T, I, Q = 512, 1024, 512, 128
+FLOPS = 2 * 2 * D * T * Q
+
+F32 = mybir.dt.float32
+BF16 = mybir.dt.bfloat16
+I32 = mybir.dt.int32
+U32 = mybir.dt.uint32
+U16 = mybir.dt.uint16
+U8 = mybir.dt.uint8
+FP8X4 = mybir.dt.float8_e4m3fn_x4
+FP4X4 = mybir.dt.float4_e2m1fn_x4
+ALU = mybir.AluOpType
+ACT = mybir.ActivationFunctionType
+AX = mybir.AxisListType
+
+P = 128
+PACK = 4
+CHUNK = 256
+HALF = I // 2
+STORE = 256
+
+
+def tile_attend_planecos_twoheats_moved_heads_kernel(
+    tc, query, query2, keys_words, keys_scales, lam, sharp, share, old, gainm, offs, offs2, offs4, out
+):
+    nc = tc.nc
+    with ExitStack() as ctx:
+        sb = ctx.enter_context(tc.tile_pool(name="sb", bufs=1))
+        ps = ctx.enter_context(tc.psum_pool(name="ps", bufs=1))
+
+        def wide(name, cols=I, tag=None):
+            return sb.tile([P, cols], F32, name=name, tag=tag or name, align_bytes=64)
+
+        def column(name):
+            return sb.tile([P, 1], F32, name=name)
+
+        key_scales = sb.tile([P, T], U8, name="key_scales", align_bytes=64)
+        nc.gpsimd.memset(key_scales[:].bitcast(I32), 0)
+        placed = wide("placed", T)
+        nc.gpsimd.memset(placed[:], 0.0)
+
+        raw_a = sb.tile([P, PACK, Q], F32, name="raw_a", align_bytes=64)
+        raw_b = sb.tile([P, PACK, Q], F32, name="raw_b", align_bytes=64)
+        key_words = [sb.tile([P, T], U8, name="key_words%d" % h, tag="key_words%d" % h, align_bytes=64) for h in range(2)]
+        nc.sync.dma_start(out=raw_a[:], in_=query.rearrange("(p j) w -> p j w", j=PACK))
+        nc.sync.dma_start(out=raw_b[:], in_=query2.rearrange("(p j) w -> p j w", j=PACK))
+        for quad in range(4):
+            nc.sync.dma_start(
+                out=key_scales[32 * quad : 32 * quad + 4, :].bitcast(I32),
+                in_=keys_scales[0, 4 * quad : 4 * quad + 4, :].bitcast(I32),
+            )
+        nc.sync.dma_start(out=key_words[0][:].bitcast(I32), in_=keys_words[0, :, :T].bitcast(I32))
+        nc.sync.dma_start(out=key_words[1][:].bitcast(I32), in_=keys_words[0, :, T:].bitcast(I32))
+        list1 = sb.tile([P, I // 16], U16, name="list1")
+        list2 = sb.tile([P, I // 16], U16, name="list2")
+        list4 = sb.tile([P, I // 16], U16, name="list4")
+        nc.sync.dma_start(list1[:], offs)
+        nc.sync.dma_start(list2[:], offs2)
+        gain = wide("gain")
+        nc.sync.dma_start(out=gain[:], in_=gainm)
+        share_c, lam_c, sharp_c = column("share_c"), column("lam_c"), column("sharp_c")
+        nc.sync.dma_start(out=share_c[:], in_=share)
+        nc.sync.dma_start(out=lam_c[:], in_=lam)
+        nc.sync.dma_start(out=sharp_c[:], in_=sharp)
+        nc.sync.dma_start(list4[:], offs4)
+        counts = wide("counts", T)
+        nc.sync.dma_start(out=counts[:], in_=old)
+
+        def quantised(name, raw, copy):
+            grouped = sb.tile([P, Q, PACK], BF16, name=name + "_grouped", align_bytes=64)
+            copy(
+                out=grouped[:].rearrange("p (c i) t -> p c t i", i=4),
+                in_=raw[:].rearrange("p t (c i) -> p c t i", i=4),
+            )
+            codes = sb.tile([P, Q], U32, name=name + "_codes", align_bytes=64)
+            scales = sb.tile([P, Q], U8, name=name + "_scales", align_bytes=64)
+            nc.vector.quantize_mx(
+                out=codes[:].bitcast(FP8X4), scales=scales[:], in_=grouped[:].rearrange("p w j -> p (w j)")
+            )
+            return codes, scales
+
+        def product(name, codes, scales, copies):
+            whole = wide(name, T)
+            for n, copy in enumerate(copies):
+                bank = ps.tile([P, 512], F32, name=name + "_bank%d" % n)
+                cols = slice(n * CHUNK, (n + 1) * CHUNK)
+                first = 2 * CHUNK * (n % 2)
+                nc.tensor.matmul_mx(
+                    out=bank[:, :CHUNK],
+                    lhsT=codes[:].bitcast(FP8X4),
+                    lhsT_scale=scales[:],
+                    rhs=key_words[n // 2][:, first : first + 2 * CHUNK].bitcast(FP4X4),
+                    rhs_scale=key_scales[:, cols],
+                    start=True,
+                    stop=True,
+                )
+                copy(out=whole[:, cols], in_=bank[:, :CHUNK])
+            return whole
+
+        codes_a, scales_a = quantised("qa", raw_a, nc.vector.tensor_copy)
+        codes_b, scales_b = quantised("qb", raw_b, nc.vector.tensor_copy)
+        a = product("a", codes_a, scales_a, [nc.vector.tensor_copy, nc.scalar.copy] * 2)
+        b = product("b", codes_b, scales_b, [nc.scalar.copy] * 4)
+
+        share_less = column("share_less")
+        nc.gpsimd.tensor_scalar(share_less[:], share_c[:], -1.0, 1.0, ALU.add, ALU.mult)
+        sharp_neg = column("sharp_neg")
+        nc.gpsimd.tensor_scalar(sharp_neg[:], sharp_c[:], -1.0, 0.0, ALU.mult, ALU.add)
+
+        a1, b1, a2, b2 = wide("a1"), wide("b1"), wide("a2", tag="key_words1"), wide("b2")
+        nc.vector.tensor_copy(a1[:], a[:].indirect(list1[:]))
+        nc.scalar.activation(a2[:], a[:].indirect(list2[:]), ACT.Copy)
+        nc.vector.tensor_copy(b1[:], b[:].indirect(list1[:]))
+        nc.scalar.activation(b2[:], b[:].indirect(list2[:]), ACT.Copy)
+
+        halves = [slice(0, HALF), slice(HALF, I)]
+        a1s, b1s, a2s, b2s = wide("a1s"), wide("b1s"), wide("a2s"), wide("b2s")
+        la, lb, lab, aa, bb, dot = (wide(n) for n in ("la", "lb", "lab", "aa", "bb", "dot"))
+        inv_len, s, s2_neg = wide("inv_len"), wide("s"), wide("s2_neg")
+        nc.vector.tensor_tensor(a1s[:], a1[:], a1[:], ALU.mult)
+        nc.scalar.activation(b1s[:], b1[:], ACT.Square)
+        nc.scalar.activation(a2s[:], a2[:], ACT.Square)
+        for h in halves:
+            nc.scalar.activation(b2s[:, h], b2[:, h], ACT.Square)
+        nc.vector.tensor_tensor(aa[:], a1[:], a2[:], ALU.mult)
+        nc.vector.tensor_tensor(bb[:], b1[:], b2[:], ALU.mult)
+        nc.vector.tensor_tensor(la[:], a1s[:], b1s[:], ALU.add)
+        nc.vector.tensor_tensor(dot[:, halves[0]], aa[:, halves[0]], bb[:, halves[0]], ALU.add)
+        for h in halves:
+            nc.vector.tensor_tensor(lb[:, h], a2s[:, h], b2s[:, h], ALU.add)
+        for h in halves:
+            nc.vector.tensor_tensor(lab[:, h], la[:, h], lb[:, h], ALU.mult)
+        nc.vector.tensor_tensor(dot[:, halves[1]], aa[:, halves[1]], bb[:, halves[1]], ALU.add)
+        for h in halves:
+            nc.scalar.activation(inv_len[:, h], lab[:, h], ACT.Abs_reciprocal_sqrt, bias=0.5)
+        top1_neg, top2_neg = column("top1_neg"), column("top2_neg")
+        for h in halves:
+            nc.vector.scalar_tensor_tensor(s[:, h], dot[:, h], lam_c[:], inv_len[:, h], ALU.mult, ALU.mult)
+        gain1, gain2 = wide("gain1", tag="inv_len"), wide("gain2", tag="dot")
+        nc.gpsimd.tensor_scalar(gain1[:], gain[:], share_c[:], 256.0, ALU.mult, ALU.mult)
+        nc.gpsimd.tensor_scalar(gain2[:], gain[:], share_less[:], 256.0, ALU.mult, ALU.mult)
+        nc.vector.tensor_reduce(top1_neg[:], s[:], AX.X, ALU.max, negate=True)
+        nc.vector.tensor_scalar(s2_neg[:], s[:], sharp_neg[:], None, ALU.mult, ALU.min, accum_out=top2_neg[:])
+
+        p1, p2 = wide("p1"), wide("p2")
+        sums = sb.tile([P, 2], F32, name="sums")
+        nc.scalar.activation(p1[:], s[:], ACT.Exp, bias=top1_neg[:], accum_out=sums[:, 0:1])
+        nc.scalar.activation(p2[:], s2_neg[:], ACT.Exp, bias=top2_neg[:], scale=-1.0, accum_out=sums[:, 1:2])
+        p1g, part1, part2 = wide("p1g"), wide("part1"), wide("part2")
+        nc.vector.tensor_tensor(p1g[:], p1[:], gain1[:], ALU.mult)
+        inv_sums = sb.tile([P, 2], F32, name="inv_sums")
+        nc.vector.reciprocal(inv_sums[:], sums[:])
+        nc.scalar.activation(part1[:], p1g[:], ACT.Copy, scale=inv_sums[:, 0:1])
+        nc.vector.scalar_tensor_tensor(part2[:], p2[:], inv_sums[:, 1:2], gain2[:], ALU.mult, ALU.mult)
+        nc.vector.tensor_tensor(placed[:].indirect(list4[:]), part1[:], part2[:], ALU.add)
+
+        for n in range(T // STORE):
+            cols = slice(n * STORE, (n + 1) * STORE)
+            piece = wide("piece%d" % n, STORE)
+            nc.vector.tensor_tensor(piece[:], placed[:, cols], counts[:, cols], ALU.add)
+            (nc.sync if n % 2 == 0 else nc.scalar).dma_start(out=out[:, cols], in_=piece[:])

@@ -121,20 +121,21 @@ def tile_attend_planecos_twoheats_moved_heads_kernel(
         a1s, b1s, a2s, b2s = wide("a1s"), wide("b1s"), wide("a2s"), wide("b2s")
         la, lb, lab, aa, bb, dot = (wide(n) for n in ("la", "lb", "lab", "aa", "bb", "dot"))
         inv_len, s, s2_neg = wide("inv_len"), wide("s"), wide("s2_neg")
-        nc.vector.tensor_tensor(a1s[:], a1[:], a1[:], ALU.mult)
-        nc.scalar.activation(b1s[:], b1[:], ACT.Square)
+        nc.gpsimd.tensor_tensor(a1s[:], a1[:], a1[:], ALU.mult)
+        nc.vector.tensor_tensor(b1s[:], b1[:], b1[:], ALU.mult)
         nc.scalar.activation(a2s[:], a2[:], ACT.Square)
         for h in halves:
             nc.scalar.activation(b2s[:, h], b2[:, h], ACT.Square)
-        nc.vector.tensor_tensor(aa[:], a1[:], a2[:], ALU.mult)
-        nc.vector.tensor_tensor(bb[:], b1[:], b2[:], ALU.mult)
         nc.vector.tensor_tensor(la[:], a1s[:], b1s[:], ALU.add)
-        nc.vector.tensor_tensor(dot[:, halves[0]], aa[:, halves[0]], bb[:, halves[0]], ALU.add)
         for h in halves:
             nc.vector.tensor_tensor(lb[:, h], a2s[:, h], b2s[:, h], ALU.add)
         for h in halves:
             nc.vector.tensor_tensor(lab[:, h], la[:, h], lb[:, h], ALU.mult)
-        nc.vector.tensor_tensor(dot[:, halves[1]], aa[:, halves[1]], bb[:, halves[1]], ALU.add)
+        for h in halves:
+            nc.vector.tensor_tensor(aa[:, h], a1[:, h], a2[:, h], ALU.mult)
+        nc.vector.tensor_tensor(bb[:], b1[:], b2[:], ALU.mult)
+        for h in halves:
+            nc.vector.tensor_tensor(dot[:, h], aa[:, h], bb[:, h], ALU.add)
         for h in halves:
             nc.scalar.activation(inv_len[:, h], lab[:, h], ACT.Abs_reciprocal_sqrt, bias=0.5)
         top1_neg, top2_neg = column("top1_neg"), column("top2_neg")

@@ -43,6 +43,10 @@ def tile_attend_planecos_twoheats_moved_heads_kernel(
         placed = wide("placed", T)
         nc.gpsimd.memset(placed[:], 0.0)
 
+        warm_in, warm_out = column("warm_in"), column("warm_out")
+        nc.vector.memset(warm_in[:], 1.0)
+        nc.scalar.activation(warm_out[:], warm_in[:], ACT.Abs_reciprocal_sqrt)
+
         raw_a = sb.tile([P, PACK, Q], F32, name="raw_a", align_bytes=64)
         raw_b = sb.tile([P, PACK, Q], F32, name="raw_b", align_bytes=64)
         key_words = [sb.tile([P, T], U8, name="key_words%d" % h, tag="key_words%d" % h, align_bytes=64) for h in range(2)]

from contextlib import ExitStack

import concourse.mybir as mybir

D, T, I, Q = 512, 1024, 512, 128
FLOPS = 2 * 2 * D * T * Q

F32 = mybir.dt.float32
BF16 = mybir.dt.bfloat16
I32 = mybir.dt.int32
U32 = mybir.dt.uint32
U16 = mybir.dt.uint16
U8 = mybir.dt.uint8
FP8X4 = mybir.dt.float8_e4m3fn_x4
FP4X4 = mybir.dt.float4_e2m1fn_x4
ALU = mybir.AluOpType
ACT = mybir.ActivationFunctionType
AX = mybir.AxisListType

P = 128
PACK = 4
CHUNK = 256
HALF = I // 2
STORE = 256


def tile_attend_planecos_twoheats_moved_heads_kernel(
    tc, query, query2, keys_words, keys_scales, lam, sharp, share, old, gainm, offs, offs2, offs4, out
):
    nc = tc.nc
    with ExitStack() as ctx:
        sb = ctx.enter_context(tc.tile_pool(name="sb", bufs=1))
        ps = ctx.enter_context(tc.psum_pool(name="ps", bufs=1))

        def wide(name, cols=I, tag=None):
            return sb.tile([P, cols], F32, name=name, tag=tag or name, align_bytes=64)

        def column(name):
            return sb.tile([P, 1], F32, name=name)

        key_scales = sb.tile([P, T], U8, name="key_scales", align_bytes=64)
        nc.gpsimd.memset(key_scales[:].bitcast(I32), 0)
        placed = wide("placed", T)
        nc.gpsimd.memset(placed[:], 0.0)

        warm_in, warm_out = column("warm_in"), column("warm_out")
        nc.vector.memset(warm_in[:], 1.0)
        nc.scalar.activation(warm_out[:], warm_in[:], ACT.Abs_reciprocal_sqrt)

        raw_a = sb.tile([P, PACK, Q], F32, name="raw_a", align_bytes=64)
        raw_b = sb.tile([P, PACK, Q], F32, name="raw_b", align_bytes=64)
        key_words = [sb.tile([P, T], U8, name="key_words%d" % h, tag="key_words%d" % h, align_bytes=64) for h in range(2)]
        nc.sync.dma_start(out=raw_a[:], in_=query.rearrange("(p j) w -> p j w", j=PACK))
        nc.sync.dma_start(out=raw_b[:], in_=query2.rearrange("(p j) w -> p j w", j=PACK))
        for quad in range(4):
            nc.sync.dma_start(
                out=key_scales[32 * quad : 32 * quad + 4, :].bitcast(I32),
                in_=keys_scales[0, 4 * quad : 4 * quad + 4, :].bitcast(I32),
            )
        nc.sync.dma_start(out=key_words[0][:].bitcast(I32), in_=keys_words[0, :, :T].bitcast(I32))
        nc.sync.dma_start(out=key_words[1][:].bitcast(I32), in_=keys_words[0, :, T:].bitcast(I32))
        list1 = sb.tile([P, I // 16], U16, name="list1")
        list2 = sb.tile([P, I // 16], U16, name="list2")
        list4 = sb.tile([P, I // 16], U16, name="list4")
        nc.sync.dma_start(list1[:], offs)
        nc.sync.dma_start(list2[:], offs2)
        gain = wide("gain")
        nc.sync.dma_start(out=gain[:], in_=gainm)
        share_c, lam_c, sharp_c = column("share_c"), column("lam_c"), column("sharp_c")
        nc.sync.dma_start(out=share_c[:], in_=share)
        nc.sync.dma_start(out=lam_c[:], in_=lam)
        nc.sync.dma_start(out=sharp_c[:], in_=sharp)
        nc.sync.dma_start(list4[:], offs4)
        counts = wide("counts", T)
        nc.sync.dma_start(out=counts[:], in_=old)

        def quantised(name, raw, copy):
            grouped = sb.tile([P, Q, PACK], BF16, name=name + "_grouped", align_bytes=64)
            copy(
                out=grouped[:].rearrange("p (c i) t -> p c t i", i=4),
                in_=raw[:].rearrange("p t (c i) -> p c t i", i=4),
            )
            codes = sb.tile([P, Q], U32, name=name + "_codes", align_bytes=64)
            scales = sb.tile([P, Q], U8, name=name + "_scales", align_bytes=64)
            nc.vector.quantize_mx(
                out=codes[:].bitcast(FP8X4), scales=scales[:], in_=grouped[:].rearrange("p w j -> p (w j)")
            )
            return codes, scales

        def product(name, codes, scales, copies):
            whole = wide(name, T)
            for n, copy in enumerate(copies):
                bank = ps.tile([P, 512], F32, name=name + "_bank%d" % n)
                cols = slice(n * CHUNK, (n + 1) * CHUNK)
                first = 2 * CHUNK * (n % 2)
                nc.tensor.matmul_mx(
                    out=bank[:, :CHUNK],
                    lhsT=codes[:].bitcast(FP8X4),
                    lhsT_scale=scales[:],
                    rhs=key_words[n // 2][:, first : first + 2 * CHUNK].bitcast(FP4X4),
                    rhs_scale=key_scales[:, cols],
                    start=True,
                    stop=True,
                )
                copy(out=whole[:, cols], in_=bank[:, :CHUNK])
            return whole

        codes_a, scales_a = quantised("qa", raw_a, nc.vector.tensor_copy)
        codes_b, scales_b = quantised("qb", raw_b, nc.vector.tensor_copy)
        a = product("a", codes_a, scales_a, [nc.vector.tensor_copy, nc.scalar.copy] * 2)
        b = product("b", codes_b, scales_b, [nc.scalar.copy] * 4)

        share_less = column("share_less")
        nc.gpsimd.tensor_scalar(share_less[:], share_c[:], -1.0, 1.0, ALU.add, ALU.mult)
        sharp_neg = column("sharp_neg")
        nc.gpsimd.tensor_scalar(sharp_neg[:], sharp_c[:], -1.0, 0.0, ALU.mult, ALU.add)

        a1, b1, a2, b2 = wide("a1"), wide("b1"), wide("a2", tag="key_words1"), wide("b2")
        nc.vector.tensor_copy(a1[:], a[:].indirect(list1[:]))
        nc.scalar.activation(a2[:], a[:].indirect(list2[:]), ACT.Copy)
        nc.vector.tensor_copy(b1[:], b[:].indirect(list1[:]))
        nc.scalar.activation(b2[:], b[:].indirect(list2[:]), ACT.Copy)

        halves = [slice(0, HALF), slice(HALF, I)]
        a1s, b1s, a2s, b2s = wide("a1s"), wide("b1s"), wide("a2s"), wide("b2s")
        la, lb, lab, aa, bb, dot = (wide(n) for n in ("la", "lb", "lab", "aa", "bb", "dot"))
        inv_len, s, s2_neg = wide("inv_len"), wide("s"), wide("s2_neg")
        nc.gpsimd.tensor_tensor(a1s[:], a1[:], a1[:], ALU.mult)
        nc.vector.tensor_tensor(b1s[:], b1[:], b1[:], ALU.mult)
        nc.scalar.activation(a2s[:], a2[:], ACT.Square)
        for h in halves:
            nc.scalar.activation(b2s[:, h], b2[:, h], ACT.Square)
        nc.vector.tensor_tensor(la[:], a1s[:], b1s[:], ALU.add)
        for h in halves:
            nc.vector.tensor_tensor(lb[:, h], a2s[:, h], b2s[:, h], ALU.add)
        for h in halves:
            nc.vector.tensor_tensor(lab[:, h], la[:, h], lb[:, h], ALU.mult)
        for h in halves:
            nc.vector.tensor_tensor(aa[:, h], a1[:, h], a2[:, h], ALU.mult)
        nc.vector.tensor_tensor(bb[:], b1[:], b2[:], ALU.mult)
        for h in halves:
            nc.vector.tensor_tensor(dot[:, h], aa[:, h], bb[:, h], ALU.add)
        for h in halves:
            nc.scalar.activation(inv_len[:, h], lab[:, h], ACT.Abs_reciprocal_sqrt, bias=0.5)
        top1_neg, top2_neg = column("top1_neg"), column("top2_neg")
        for h in halves:
            nc.vector.scalar_tensor_tensor(s[:, h], dot[:, h], lam_c[:], inv_len[:, h], ALU.mult, ALU.mult)
        gain1, gain2 = wide("gain1", tag="inv_len"), wide("gain2", tag="dot")
        nc.gpsimd.tensor_scalar(gain1[:], gain[:], share_c[:], 256.0, ALU.mult, ALU.mult)
        nc.gpsimd.tensor_scalar(gain2[:], gain[:], share_less[:], 256.0, ALU.mult, ALU.mult)
        nc.vector.tensor_reduce(top1_neg[:], s[:], AX.X, ALU.max, negate=True)
        nc.vector.tensor_scalar(s2_neg[:], s[:], sharp_neg[:], None, ALU.mult, ALU.min, accum_out=top2_neg[:])

        p1, p2 = wide("p1"), wide("p2")
        sums = sb.tile([P, 2], F32, name="sums")
        nc.scalar.activation(p1[:], s[:], ACT.Exp, bias=top1_neg[:], accum_out=sums[:, 0:1])
        nc.scalar.activation(p2[:], s2_neg[:], ACT.Exp, bias=top2_neg[:], scale=-1.0, accum_out=sums[:, 1:2])
        p1g, part1, part2 = wide("p1g"), wide("part1"), wide("part2")
        nc.vector.tensor_tensor(p1g[:], p1[:], gain1[:], ALU.mult)
        inv_sums = sb.tile([P, 2], F32, name="inv_sums")
        nc.vector.reciprocal(inv_sums[:], sums[:])
        nc.scalar.activation(part1[:], p1g[:], ACT.Copy, scale=inv_sums[:, 0:1])
        nc.vector.scalar_tensor_tensor(part2[:], p2[:], inv_sums[:, 1:2], gain2[:], ALU.mult, ALU.mult)
        nc.vector.tensor_tensor(placed[:].indirect(list4[:]), part1[:], part2[:], ALU.add)

        for n in range(T // STORE):
            cols = slice(n * STORE, (n + 1) * STORE)
            piece = wide("piece%d" % n, STORE)
            nc.vector.tensor_tensor(piece[:], placed[:, cols], counts[:, cols], ALU.add)
            (nc.sync if n % 2 == 0 else nc.scalar).dma_start(out=out[:, cols], in_=piece[:])
